import numpy as np, ml_dtypes
CORES = [65,66,69,71,193,194,197,199,321,322,325,327,449,450,453,455]
N = 16
TK, LAY = 512, 4
def setup_inputs(rng):
    return {"x": rng.standard_normal((N, 128, TK), dtype=np.float32).astype(ml_dtypes.bfloat16), "w": (rng.standard_normal((N, 128, LAY * 256), dtype=np.float32) / 16).astype(ml_dtypes.bfloat16)}
def setup_inputs_big(rng):
    d = setup_inputs(rng)
    for k in ("x",): d[k] = (d[k].astype(np.float32) * 1048576.0).astype(d[k].dtype)
    return d
def setup_inputs_small(rng):
    d = setup_inputs(rng)
    for k in ("x",): d[k] = (d[k].astype(np.float32) * (1 / 1048576.0)).astype(d[k].dtype)
    return d
def setup_inputs_apart(rng):
    d = setup_inputs(rng)
    f = (10.0 ** rng.permutation(np.linspace(-1.5, 1.5, N))).astype(np.float32).reshape(N, 1, 1)
    for k in ("x",): d[k] = (d[k].astype(np.float32) * f).astype(d[k].dtype)
    return d
def reference(x, w):
    X, W = x.astype(np.float64), w.astype(np.float64)
    h = list(X)
    for l in range(LAY):
        h = [np.maximum(W[r][:, 256 * l:256 * l + 128].T @ h[r] + W[r][:, 256 * l + 128:256 * l + 256].T @ h[r ^ (1 << l)], 0.0) for r in range(N)]
    return {"y": np.stack(h).astype(ml_dtypes.bfloat16)}

@@ -1,0 +1,139 @@
+from concourse.mybir import AluOpType
+
+TK, LAY = 512, 4
+NCH = 2
+CW = TK // NCH
+NBANK = 8
+
+SCRATCH = {"zero": ("sbuf", [128, CW], "float32"),
+           "wp": ("sbuf", [128, 256], "bfloat16")}
+for _l in range(LAY):
+    SCRATCH["w%d" % _l] = ("sbuf", [128, 256], "bfloat16")
+    for _c in range(NCH):
+        SCRATCH["h%d_%d" % (_l, _c)] = ("sbuf", [128, CW], "bfloat16")
+        SCRATCH["in%d_%d" % (_l, _c)] = ("sbuf", [128, CW], "bfloat16")
+for _c in range(NCH):
+    SCRATCH["hp_%d" % _c] = ("sbuf", [128, CW], "bfloat16")
+    SCRATCH["h4_%d" % _c] = ("sbuf", [128, CW], "bfloat16")
+for _b in range(NBANK):
+    SCRATCH["ps%d" % _b] = ("psum", [128, 512], "float32")
+
+SEMAPHORES = ["zr", "sent", "arrw"]
+for _l in range(LAY):
+    SEMAPHORES.append("ldw%d" % _l)
+    for _c in range(NCH):
+        SEMAPHORES += ["arr%d_%d" % (_l, _c), "mm%d_%d" % (_l, _c), "rdy%d_%d" % (_l, _c)]
+for _c in range(NCH):
+    SEMAPHORES += ["mmp_%d" % _c, "rdyp_%d" % _c, "rdy4_%d" % _c, "st_%d" % _c]
+
+
+def _bits(m):
+    return bin(m).count("1")
+
+
+def rank_program(g, core, T, topo):
+    r = T.rank_of(core)
+    if r is None:
+        return
+    cores, S = T.cores, T.sem
+    te, ve = g.tensor, g.vector
+    lq = [g.sync, g.scalar]
+
+    def feeder(d):
+        p = d ^ 8
+        for q in (p, p ^ 4):
+            if topo.may_write(cores[q], cores[d]):
+                return q
+        return None
+
+    def mask(l, c, src, dst):
+        full = topo.mask(cores[src], cores[dst])
+        if l == 0:
+            off = topo.mask(cores[src], cores[src ^ 4])
+            return (full & ~off) if c % 2 == 0 else (full & off)
+        return full
+
+    sent = [0]
+
+    def send(dst, out, src_ap, sem, m):
+        rid, pid = topo.addr(cores[dst], core)
+        g.remote_dma(out_ap=out, in_ap=src_ap, remote_sem=sem, local_sem=S.sent, pid=pid, routing_id=rid, dma_engine_mask=m)
+        sent[0] += _bits(m)
+
+    for c in range(NCH):
+        lq[c % 2].dma_start(T["h0_%d" % c][:], T.x[:, c * CW:(c + 1) * CW]).then_inc(S["rdy0_%d" % c], 16)
+    for q, l in ((0, 0), (1, 2), (0, 1), (1, 3)):
+        lq[q].dma_start(T["w%d" % l][:], T.w[:, 256 * l:256 * (l + 1)]).then_inc(S["ldw%d" % l], 16)
+    ve.memset(T.zero[:], 0.0).then_inc(S.zr, 1)
+
+    def ready(l):
+        return 16 if l == 0 else 1
+
+    for l in range(LAY):
+        for c in range(NCH):
+            if l < 3:
+                p = r ^ (1 << l)
+                g.wait_ge(S["rdy%d_%d" % (l, c)], ready(l))
+                send(p, T["in%d_%d" % (l, c)][:], T["h%d_%d" % (l, c)][:], S["arr%d_%d" % (l, c)], mask(l, c, r, p))
+            else:
+                for d in range(len(cores)):
+                    if feeder(d) == r:
+                        own = (d ^ 8) == r
+                        g.wait_ge(S[("rdy3_%d" if own else "rdyp_%d") % c], 1)
+                        send(d, T["in3_%d" % c][:], T[("h3_%d" if own else "hp_%d") % c][:], S["arr3_%d" % c], mask(l, c, r, d))
+        if l == 0:
+            g.wait_ge(S.ldw2, 16)
+            send(r ^ 4, T.wp[:], T.w2[:], S.arrw, topo.mask(core, cores[r ^ 4]))
+    g.wait_ge(S.sent, sent[0])
+
+    nxt = [0]
+    last = {}
+
+    def bank(done_sem):
+        b = nxt[0] % NBANK
+        nxt[0] += 1
+        if b in last:
+            te.wait_ge(S[last[b]], 1)
+        last[b] = done_sem
+        return T["ps%d" % b][:, 0:CW]
+
+    ps, psp = {}, {}
+    for l in range(LAY):
+        u, v = T["w%d" % l][:, 0:128], T["w%d" % l][:, 128:256]
+        te.wait_ge(S["ldw%d" % l], 16)
+        for c in range(NCH):
+            te.wait_ge(S["rdy%d_%d" % (l, c)], ready(l))
+            ps[l, c] = bank("rdy%d_%d" % (l + 1, c))
+            te.matmul(ps[l, c], u, T["h%d_%d" % (l, c)][:], True, False)
+        if l == 2:
+            te.wait_ge(S.arrw, _bits(topo.mask(cores[r ^ 4], core)))
+            for c in range(NCH):
+                psp[c] = bank("rdyp_%d" % c)
+                te.matmul(psp[c], T.wp[:, 128:256], T["h2_%d" % c][:], True, False)
+        src = feeder(r) if l == 3 else r ^ (1 << l)
+        for c in range(NCH):
+            te.wait_ge(S["arr%d_%d" % (l, c)], _bits(mask(l, c, src, r)))
+            if l == 2:
+                te.matmul(psp[c], T.wp[:, 0:128], T["in2_%d" % c][:], False, True).then_inc(S["mmp_%d" % c], 1)
+            else:
+                te.matmul(ps[l, c], v, T["in%d_%d" % (l, c)][:], False, True).then_inc(S["mm%d_%d" % (l, c)], 1)
+        if l == 2:
+            for c in range(NCH):
+                te.matmul(ps[l, c], v, T["in2_%d" % c][:], False, True).then_inc(S["mm2_%d" % c], 1)
+
+    ve.wait_ge(S.zr, 1)
+    for l in range(LAY):
+        if l == 2:
+            for c in range(NCH):
+                ve.wait_ge(S["mmp_%d" % c], 1)
+                ve.tensor_tensor(T["hp_%d" % c][:], psp[c], T.zero[:], AluOpType.max).then_inc(S["rdyp_%d" % c], 1)
+        for c in range(NCH):
+            ve.wait_ge(S["mm%d_%d" % (l, c)], 1)
+            ve.tensor_tensor(T["h%d_%d" % (l + 1, c)][:], ps[l, c], T.zero[:], AluOpType.max).then_inc(S["rdy%d_%d" % (l + 1, c)], 1)
+
+    for c in range(NCH):
+        q = lq[c % 2]
+        q.wait_ge(S["rdy4_%d" % c], 1)
+        q.dma_start(T.y[:, c * CW:(c + 1) * CW], T["h4_%d" % c][:]).then_inc(S["st_%d" % c], 16)
+    for c in range(NCH):
+        lq[c % 2].wait_ge(S["st_%d" % c], 16)

@@ -1,20 +1,21 @@
 from concourse.mybir import AluOpType
 
 TK, LAY = 512, 4
-NCH = 2
-CW = TK // NCH
+WIDTHS = [128, 128, 128, 128]
+NCH = len(WIDTHS)
+OFFS = [sum(WIDTHS[:_c]) for _c in range(NCH)]
 NBANK = 8
 
-SCRATCH = {"zero": ("sbuf", [128, CW], "float32"),
+SCRATCH = {"zero": ("sbuf", [128, max(WIDTHS)], "float32"),
            "wp": ("sbuf", [128, 256], "bfloat16")}
 for _l in range(LAY):
     SCRATCH["w%d" % _l] = ("sbuf", [128, 256], "bfloat16")
     for _c in range(NCH):
-        SCRATCH["h%d_%d" % (_l, _c)] = ("sbuf", [128, CW], "bfloat16")
-        SCRATCH["in%d_%d" % (_l, _c)] = ("sbuf", [128, CW], "bfloat16")
+        SCRATCH["h%d_%d" % (_l, _c)] = ("sbuf", [128, WIDTHS[_c]], "bfloat16")
+        SCRATCH["in%d_%d" % (_l, _c)] = ("sbuf", [128, WIDTHS[_c]], "bfloat16")
 for _c in range(NCH):
-    SCRATCH["hp_%d" % _c] = ("sbuf", [128, CW], "bfloat16")
-    SCRATCH["h4_%d" % _c] = ("sbuf", [128, CW], "bfloat16")
+    SCRATCH["hp_%d" % _c] = ("sbuf", [128, WIDTHS[_c]], "bfloat16")
+    SCRATCH["h4_%d" % _c] = ("sbuf", [128, WIDTHS[_c]], "bfloat16")
 for _b in range(NBANK):
     SCRATCH["ps%d" % _b] = ("psum", [128, 512], "float32")
 
@@ -46,23 +47,20 @@ def rank_program(g, core, T, topo):
                 return q
         return None
 
-    def mask(l, c, src, dst):
-        full = topo.mask(cores[src], cores[dst])
-        if l == 0:
-            off = topo.mask(cores[src], cores[src ^ 4])
-            return (full & ~off) if c % 2 == 0 else (full & off)
-        return full
+    def mask(src, dst):
+        return topo.mask(cores[src], cores[dst])
 
     sent = [0]
 
-    def send(dst, out, src_ap, sem, m):
+    def send(dst, out, src_ap, sem):
         rid, pid = topo.addr(cores[dst], core)
+        m = mask(r, dst)
         g.remote_dma(out_ap=out, in_ap=src_ap, remote_sem=sem, local_sem=S.sent, pid=pid, routing_id=rid, dma_engine_mask=m)
         sent[0] += _bits(m)
 
     for c in range(NCH):
-        lq[c % 2].dma_start(T["h0_%d" % c][:], T.x[:, c * CW:(c + 1) * CW]).then_inc(S["rdy0_%d" % c], 16)
-    for q, l in ((0, 0), (1, 2), (0, 1), (1, 3)):
+        lq[c % 2].dma_start(T["h0_%d" % c][:], T.x[:, OFFS[c]:OFFS[c] + WIDTHS[c]]).then_inc(S["rdy0_%d" % c], 16)
+    for q, l in ((NCH % 2, 0), ((NCH + 1) % 2, 2), (NCH % 2, 1), ((NCH + 1) % 2, 3)):
         lq[q].dma_start(T["w%d" % l][:], T.w[:, 256 * l:256 * (l + 1)]).then_inc(S["ldw%d" % l], 16)
     ve.memset(T.zero[:], 0.0).then_inc(S.zr, 1)
 
@@ -72,30 +70,29 @@ def rank_program(g, core, T, topo):
     for l in range(LAY):
         for c in range(NCH):
             if l < 3:
-                p = r ^ (1 << l)
                 g.wait_ge(S["rdy%d_%d" % (l, c)], ready(l))
-                send(p, T["in%d_%d" % (l, c)][:], T["h%d_%d" % (l, c)][:], S["arr%d_%d" % (l, c)], mask(l, c, r, p))
+                send(r ^ (1 << l), T["in%d_%d" % (l, c)][:], T["h%d_%d" % (l, c)][:], S["arr%d_%d" % (l, c)])
             else:
                 for d in range(len(cores)):
                     if feeder(d) == r:
                         own = (d ^ 8) == r
                         g.wait_ge(S[("rdy3_%d" if own else "rdyp_%d") % c], 1)
-                        send(d, T["in3_%d" % c][:], T[("h3_%d" if own else "hp_%d") % c][:], S["arr3_%d" % c], mask(l, c, r, d))
+                        send(d, T["in3_%d" % c][:], T[("h3_%d" if own else "hp_%d") % c][:], S["arr3_%d" % c])
         if l == 0:
             g.wait_ge(S.ldw2, 16)
-            send(r ^ 4, T.wp[:], T.w2[:], S.arrw, topo.mask(core, cores[r ^ 4]))
+            send(r ^ 4, T.wp[:], T.w2[:], S.arrw)
     g.wait_ge(S.sent, sent[0])
 
     nxt = [0]
     last = {}
 
-    def bank(done_sem):
+    def bank(c, done_sem):
         b = nxt[0] % NBANK
         nxt[0] += 1
         if b in last:
             te.wait_ge(S[last[b]], 1)
         last[b] = done_sem
-        return T["ps%d" % b][:, 0:CW]
+        return T["ps%d" % b][:, 0:WIDTHS[c]]
 
     ps, psp = {}, {}
     for l in range(LAY):
@@ -103,37 +100,33 @@ def rank_program(g, core, T, topo):
         te.wait_ge(S["ldw%d" % l], 16)
         for c in range(NCH):
             te.wait_ge(S["rdy%d_%d" % (l, c)], ready(l))
-            ps[l, c] = bank("rdy%d_%d" % (l + 1, c))
+            ps[l, c] = bank(c, "rdy%d_%d" % (l + 1, c))
             te.matmul(ps[l, c], u, T["h%d_%d" % (l, c)][:], True, False)
         if l == 2:
-            te.wait_ge(S.arrw, _bits(topo.mask(cores[r ^ 4], core)))
+            te.wait_ge(S.arrw, _bits(mask(r ^ 4, r)))
             for c in range(NCH):
-                psp[c] = bank("rdyp_%d" % c)
+                psp[c] = bank(c, "rdyp_%d" % c)
                 te.matmul(psp[c], T.wp[:, 128:256], T["h2_%d" % c][:], True, False)
         src = feeder(r) if l == 3 else r ^ (1 << l)
         for c in range(NCH):
-            te.wait_ge(S["arr%d_%d" % (l, c)], _bits(mask(l, c, src, r)))
+            te.wait_ge(S["arr%d_%d" % (l, c)], _bits(mask(src, r)))
             if l == 2:
                 te.matmul(psp[c], T.wp[:, 0:128], T["in2_%d" % c][:], False, True).then_inc(S["mmp_%d" % c], 1)
-            else:
-                te.matmul(ps[l, c], v, T["in%d_%d" % (l, c)][:], False, True).then_inc(S["mm%d_%d" % (l, c)], 1)
-        if l == 2:
-            for c in range(NCH):
-                te.matmul(ps[l, c], v, T["in2_%d" % c][:], False, True).then_inc(S["mm2_%d" % c], 1)
+            te.matmul(ps[l, c], v, T["in%d_%d" % (l, c)][:], False, True).then_inc(S["mm%d_%d" % (l, c)], 1)
 
     ve.wait_ge(S.zr, 1)
     for l in range(LAY):
-        if l == 2:
-            for c in range(NCH):
-                ve.wait_ge(S["mmp_%d" % c], 1)
-                ve.tensor_tensor(T["hp_%d" % c][:], psp[c], T.zero[:], AluOpType.max).then_inc(S["rdyp_%d" % c], 1)
         for c in range(NCH):
+            if l == 2:
+                ve.wait_ge(S["mmp_%d" % c], 1)
+                ve.tensor_tensor(T["hp_%d" % c][:], psp[c], T.zero[:, 0:WIDTHS[c]], AluOpType.max).then_inc(S["rdyp_%d" % c], 1)
             ve.wait_ge(S["mm%d_%d" % (l, c)], 1)
-            ve.tensor_tensor(T["h%d_%d" % (l + 1, c)][:], ps[l, c], T.zero[:], AluOpType.max).then_inc(S["rdy%d_%d" % (l + 1, c)], 1)
+            ve.tensor_tensor(T["h%d_%d" % (l + 1, c)][:], ps[l, c], T.zero[:, 0:WIDTHS[c]],
+                             AluOpType.max).then_inc(S["rdy%d_%d" % (l + 1, c)], 1)
 
     for c in range(NCH):
         q = lq[c % 2]
         q.wait_ge(S["rdy4_%d" % c], 1)
-        q.dma_start(T.y[:, c * CW:(c + 1) * CW], T["h4_%d" % c][:]).then_inc(S["st_%d" % c], 16)
+        q.dma_start(T.y[:, OFFS[c]:OFFS[c] + WIDTHS[c]], T["h4_%d" % c][:]).then_inc(S["st_%d" % c], 16)
     for c in range(NCH):
         lq[c % 2].wait_ge(S["st_%d" % c], 16)

from concourse.mybir import AluOpType

TK, LAY = 512, 4
WIDTHS = [128, 128, 128, 128]
NCH = len(WIDTHS)
OFFS = [sum(WIDTHS[:_c]) for _c in range(NCH)]
NBANK = 8

SCRATCH = {"zero": ("sbuf", [128, max(WIDTHS)], "float32"),
           "wp": ("sbuf", [128, 256], "bfloat16")}
for _l in range(LAY):
    SCRATCH["w%d" % _l] = ("sbuf", [128, 256], "bfloat16")
    for _c in range(NCH):
        SCRATCH["h%d_%d" % (_l, _c)] = ("sbuf", [128, WIDTHS[_c]], "bfloat16")
        SCRATCH["in%d_%d" % (_l, _c)] = ("sbuf", [128, WIDTHS[_c]], "bfloat16")
for _c in range(NCH):
    SCRATCH["hp_%d" % _c] = ("sbuf", [128, WIDTHS[_c]], "bfloat16")
    SCRATCH["h4_%d" % _c] = ("sbuf", [128, WIDTHS[_c]], "bfloat16")
for _b in range(NBANK):
    SCRATCH["ps%d" % _b] = ("psum", [128, 512], "float32")

SEMAPHORES = ["zr", "sent", "arrw"]
for _l in range(LAY):
    SEMAPHORES.append("ldw%d" % _l)
    for _c in range(NCH):
        SEMAPHORES += ["arr%d_%d" % (_l, _c), "mm%d_%d" % (_l, _c), "rdy%d_%d" % (_l, _c)]
for _c in range(NCH):
    SEMAPHORES += ["mmp_%d" % _c, "rdyp_%d" % _c, "rdy4_%d" % _c, "st_%d" % _c]


def _bits(m):
    return bin(m).count("1")


def rank_program(g, core, T, topo):
    r = T.rank_of(core)
    if r is None:
        return
    cores, S = T.cores, T.sem
    te, ve = g.tensor, g.vector
    lq = [g.sync, g.scalar]

    def feeder(d):
        p = d ^ 8
        for q in (p, p ^ 4):
            if topo.may_write(cores[q], cores[d]):
                return q
        return None

    def mask(src, dst):
        return topo.mask(cores[src], cores[dst])

    sent = [0]

    def send(dst, out, src_ap, sem):
        rid, pid = topo.addr(cores[dst], core)
        m = mask(r, dst)
        g.remote_dma(out_ap=out, in_ap=src_ap, remote_sem=sem, local_sem=S.sent, pid=pid, routing_id=rid, dma_engine_mask=m)
        sent[0] += _bits(m)

    for c in range(NCH):
        lq[c % 2].dma_start(T["h0_%d" % c][:], T.x[:, OFFS[c]:OFFS[c] + WIDTHS[c]]).then_inc(S["rdy0_%d" % c], 16)
    for q, l in ((NCH % 2, 0), ((NCH + 1) % 2, 2), (NCH % 2, 1), ((NCH + 1) % 2, 3)):
        lq[q].dma_start(T["w%d" % l][:], T.w[:, 256 * l:256 * (l + 1)]).then_inc(S["ldw%d" % l], 16)
    ve.memset(T.zero[:], 0.0).then_inc(S.zr, 1)

    def ready(l):
        return 16 if l == 0 else 1

    for l in range(LAY):
        for c in range(NCH):
            if l < 3:
                g.wait_ge(S["rdy%d_%d" % (l, c)], ready(l))
                send(r ^ (1 << l), T["in%d_%d" % (l, c)][:], T["h%d_%d" % (l, c)][:], S["arr%d_%d" % (l, c)])
            else:
                for d in range(len(cores)):
                    if feeder(d) == r:
                        own = (d ^ 8) == r
                        g.wait_ge(S[("rdy3_%d" if own else "rdyp_%d") % c], 1)
                        send(d, T["in3_%d" % c][:], T[("h3_%d" if own else "hp_%d") % c][:], S["arr3_%d" % c])
        if l == 0:
            g.wait_ge(S.ldw2, 16)
            send(r ^ 4, T.wp[:], T.w2[:], S.arrw)
    g.wait_ge(S.sent, sent[0])

    nxt = [0]
    last = {}

    def bank(c, done_sem):
        b = nxt[0] % NBANK
        nxt[0] += 1
        if b in last:
            te.wait_ge(S[last[b]], 1)
        last[b] = done_sem
        return T["ps%d" % b][:, 0:WIDTHS[c]]

    ps, psp = {}, {}
    for l in range(LAY):
        u, v = T["w%d" % l][:, 0:128], T["w%d" % l][:, 128:256]
        te.wait_ge(S["ldw%d" % l], 16)
        for c in range(NCH):
            te.wait_ge(S["rdy%d_%d" % (l, c)], ready(l))
            ps[l, c] = bank(c, "rdy%d_%d" % (l + 1, c))
            te.matmul(ps[l, c], u, T["h%d_%d" % (l, c)][:], True, False)
        if l == 2:
            te.wait_ge(S.arrw, _bits(mask(r ^ 4, r)))
            for c in range(NCH):
                psp[c] = bank(c, "rdyp_%d" % c)
                te.matmul(psp[c], T.wp[:, 128:256], T["h2_%d" % c][:], True, False)
        src = feeder(r) if l == 3 else r ^ (1 << l)
        for c in range(NCH):
            te.wait_ge(S["arr%d_%d" % (l, c)], _bits(mask(src, r)))
            if l == 2:
                te.matmul(psp[c], T.wp[:, 0:128], T["in2_%d" % c][:], False, True).then_inc(S["mmp_%d" % c], 1)
            te.matmul(ps[l, c], v, T["in%d_%d" % (l, c)][:], False, True).then_inc(S["mm%d_%d" % (l, c)], 1)

    ve.wait_ge(S.zr, 1)
    for l in range(LAY):
        for c in range(NCH):
            if l == 2:
                ve.wait_ge(S["mmp_%d" % c], 1)
                ve.tensor_tensor(T["hp_%d" % c][:], psp[c], T.zero[:, 0:WIDTHS[c]], AluOpType.max).then_inc(S["rdyp_%d" % c], 1)
            ve.wait_ge(S["mm%d_%d" % (l, c)], 1)
            ve.tensor_tensor(T["h%d_%d" % (l + 1, c)][:], ps[l, c], T.zero[:, 0:WIDTHS[c]],
                             AluOpType.max).then_inc(S["rdy%d_%d" % (l + 1, c)], 1)

    for c in range(NCH):
        q = lq[c % 2]
        q.wait_ge(S["rdy4_%d" % c], 1)
        q.dma_start(T.y[:, OFFS[c]:OFFS[c] + WIDTHS[c]], T["h4_%d" % c][:]).then_inc(S["st_%d" % c], 16)
    for c in range(NCH):
        lq[c % 2].wait_ge(S["st_%d" % c], 16)
